import numpy as np
import ml_dtypes


def mxq(x, axis, fmt="e4m3"):
    dtype, down = {"e4m3": (ml_dtypes.float8_e4m3fn, 7), "e5m2": (ml_dtypes.float8_e5m2, 14)}[fmt]
    v = np.moveaxis(np.asarray(x, np.float32).astype(ml_dtypes.bfloat16).astype(np.float64), axis, -1)
    blocks = v.reshape(v.shape[:-1] + (-1, 32))
    amax = np.abs(blocks).max(-1, keepdims=True)
    byte = np.maximum(np.where(amax > 0, np.frexp(amax)[1] - 1 + 127, 0) - down, 1)
    scale = np.exp2(byte - 127.0)
    codes = (blocks / scale).astype(np.float32).astype(dtype).astype(np.float64)
    return np.moveaxis((codes * scale).reshape(v.shape), -1, axis)


WIDE = False


def mx_kscale(k):
    if not WIDE:
        return np.ones(k)
    levels = np.array([10, -10, 5, -5, 0])
    if k % 512:
        return np.exp2(np.random.permutation(np.resize(levels, k // 32))).repeat(32)
    a = np.empty((k // 512, 16))
    for p in range(k // 512):
        a[p, :8] = np.random.permutation(np.resize(levels, 8))
        for g in range(8):
            far = levels[np.abs(levels - a[p, g]) >= 10]
            a[p, g + 8] = far[np.random.randint(len(far))]
    return np.exp2(a.ravel()).repeat(32)


def f64(x):
    return np.asarray(x).astype(np.float64)


def striped(idx):
    return np.tile(idx.reshape(-1, 16).T, (8, 1)).astype(np.uint16)


def unstriped(offs):
    return offs[:16].T.reshape(-1).astype(np.int64)


def striped8(idx):
    return np.concatenate([x.reshape(-1, 16).T for x in idx]).astype(np.uint16)


def runs(offs, k):
    lists = np.stack([offs[16 * r : 16 * r + 16].T.reshape(-1) for r in range(8)]).astype(np.int64)
    return lists[np.arange(k) % 512 // 64]


def pack_weight(w):
    k, n = w.shape
    w = f64(np.asarray(w, np.float32).astype(ml_dtypes.bfloat16)).reshape(k // 32, 32, n)
    amax = np.abs(w).max(1)
    byte = np.clip(np.where(amax > 0, np.frexp(amax)[1] - 1 + 127 - 7, 1), 1, 254)
    scaled = (w * np.exp2(127.0 - byte)[:, None, :]).reshape(k, n).astype(np.float32)
    words = np.ascontiguousarray(scaled.reshape(k // 512, 128, 4, n).transpose(0, 1, 3, 2)).astype(ml_dtypes.float8_e4m3fn).view(np.uint8)
    return words, np.ascontiguousarray(byte.astype(np.uint8).reshape(k // 512, 16, n))


def unpack_weight(words, scales):
    g, p, n, _ = words.shape
    vals = np.ascontiguousarray(words).view(ml_dtypes.float8_e4m3fn).astype(np.float64) * np.repeat(np.exp2(scales.astype(np.float64) - 127.0), 8, axis=1)[..., None]
    return vals.transpose(0, 1, 3, 2).reshape(g * 512, n)


K, T, S, H, W, G, U = 512, 1024, 256, 512, 128, 2048, 512


def setup_inputs():
    n = np.random.standard_normal
    s = mx_kscale(K)[:, None]
    packed_xT = pack_weight(n((K, T)) * s)
    packed_w1 = pack_weight(n((K, H)) / np.sqrt(2 * K) / s)
    packed_w2 = pack_weight(n((K, H)) / np.sqrt(2 * K) / s)
    packed_dT = pack_weight(n((K, G)) / s)
    perm = np.random.permutation(S)
    perm2 = np.random.permutation(S)
    perm3 = np.random.permutation(U)
    return {
        "x_words": packed_xT[0],
        "x_scales": packed_xT[1],
        "w1_words": packed_w1[0],
        "w1_scales": packed_w1[1],
        "w2_words": packed_w2[0],
        "w2_scales": packed_w2[1],
        "gs": (np.random.uniform(0.5, 1.5, (K, 1)) * s).astype(np.float32),
        "d_words": packed_dT[0],
        "d_scales": packed_dT[1],
        "offs": striped8(np.random.randint(0, T, (8, S))),
        "hz": striped8(np.random.randint(0, T, (8, S))),
        "n1": striped(perm[:W]),
        "n2": striped(perm[W:]),
        "n3": striped(perm2[:W]),
        "n4": striped(perm2[W:]),
        "n5": striped(np.random.permutation(S)),
        "k1": striped8(np.random.randint(0, G, (8, H))),
        "k2": striped8(np.random.randint(0, G, (8, H))),
        "two": striped(np.random.permutation(T)[:S]),
        "n6": striped(perm3[:S]),
        "n7": striped(perm3[S:]),
        "n8": striped(np.random.permutation(U)),
    }


def reference(x_words, x_scales, w1_words, w1_scales, w2_words, w2_scales, gs, d_words, d_scales, offs, hz, n1, n2, n3, n4, n5, k1, k2, two, n6, n7, n8):
    d_k1 = unpack_weight(d_words, d_scales)[np.arange(K)[:, None], runs(k1, K)]
    xq = unpack_weight(x_words, x_scales)[np.arange(K)[:, None], runs(offs, K)]
    x_hz = unpack_weight(x_words, x_scales)[np.arange(K)[:, None], runs(hz, K)]
    y = unpack_weight(w1_words, w1_scales).T @ xq + unpack_weight(w2_words, w2_scales).T @ x_hz
    pa = y[:, unstriped(n1)]
    pb = y[:, unstriped(n2)]
    ra = pb - pa
    ua = np.zeros((H, S))
    ua[:, unstriped(n3)] = ra
    ub = ua.copy()
    ub[:, unstriped(n4)] = pa
    z = f64(gs) * (np.maximum(ub, y[:, unstriped(n5)]))
    d_k2 = unpack_weight(d_words, d_scales)[np.arange(K)[:, None], runs(k2, K)]
    x_two = unpack_weight(x_words, x_scales)[:, unstriped(two)]
    h2 = 0.0625 * ((d_k1.T @ mxq(z, 0, "e4m3") + d_k2.T @ x_two))
    nw = 0.5 * h2
    ph = np.zeros((H, U))
    ph[:, unstriped(n6)] = h2
    pg = ph.copy()
    pg[:, unstriped(n7)] = nw
    return pg - pg[:, unstriped(n8)]

@@ -1,0 +1,252 @@
+from contextlib import ExitStack
+
+import concourse.mybir as mybir
+
+K, T, S, H, W, G, U = 512, 1024, 256, 512, 128, 2048, 512
+FLOPS = 4 * 2 * K * H * S
+
+F32 = mybir.dt.float32
+BF16 = mybir.dt.bfloat16
+I32 = mybir.dt.int32
+U32 = mybir.dt.uint32
+U16 = mybir.dt.uint16
+U8 = mybir.dt.uint8
+FP8X4 = mybir.dt.float8_e4m3fn_x4
+COPY = mybir.ActivationFunctionType.Copy
+
+P = 128
+PACK = 4
+TILES = H // P
+HALF = S // 2
+
+
+def words_view(ap):
+    return ap[0].rearrange("p n t -> p (n t)").bitcast(I32)
+
+
+def cols(lst, start, count):
+    return lst[:, start // 16 : (start + count) // 16]
+
+
+def tile_picked_dhhzmtcphwpagtwo_none_p_kernel(
+    tc, x_words, x_scales, w1_words, w1_scales, w2_words, w2_scales, gs, d_words, d_scales,
+    offs, hz, n1, n2, n3, n4, n5, k1, k2, two, n6, n7, n8, out,
+):
+    nc = tc.nc
+    with ExitStack() as ctx:
+        lists = ctx.enter_context(tc.tile_pool(name="lists", bufs=1))
+        keep = ctx.enter_context(tc.tile_pool(name="keep", bufs=1))
+        psum = ctx.enter_context(tc.psum_pool(name="psum", bufs=8))
+
+        def load_list(src, name):
+            tile = lists.tile(list(src.shape), U16, name=name)
+            nc.sync.dma_start(tile[:], src)
+            return tile
+
+        def zeroed(eng, width, name):
+            tile = keep.tile([P, width], U8, name=name, tag=name, align_bytes=64)
+            eng.memset(tile[:].bitcast(I32), 0)
+            return tile
+
+        def move_rows(dst, src, one, other):
+            for r in range(4):
+                eng = one if r % 2 == 0 else other
+                eng.dma_start(out=dst[r:P:32, :].bitcast(I32), in_=src[8 * r : P : 32, :].bitcast(I32))
+
+        x_sc = zeroed(nc.vector, T, "x_sc")
+        w_sc_raw = zeroed(nc.vector, H, "w_sc_raw")
+        y_planes = zeroed(nc.vector, 2 * S, "y_planes")
+        offs_t = load_list(offs, "offs_t")
+        hz_t = load_list(hz, "hz_t")
+        n1_t = load_list(n1, "n1_t")
+        n2_t = load_list(n2, "n2_t")
+        nc.scalar.dma_start(out=x_sc[0:P:8, :].bitcast(I32), in_=x_scales[0].bitcast(I32))
+        x_w = keep.tile([P, T], U32, name="x_w", align_bytes=64)
+        nc.sync.dma_start(out=x_w[:].bitcast(I32), in_=words_view(x_words))
+        w_raw = []
+        for name, src in (("w1_raw", w1_words), ("w2_raw", w2_words)):
+            tile = keep.tile([P, H], U32, name=name, align_bytes=64)
+            nc.sync.dma_start(out=tile[:].bitcast(I32), in_=words_view(src))
+            w_raw.append(tile)
+        for a, src in enumerate((w1_scales, w2_scales)):
+            for q in range(4):
+                eng = nc.sync
+                eng.dma_start(
+                    out=w_sc_raw[32 * q + 4 * a : 32 * q + 4 * a + 4, :].bitcast(I32),
+                    in_=src[0, 4 * q : 4 * q + 4, :].bitcast(I32),
+                )
+
+        y_bytes = keep.tile([P, 2 * S], U8, name="y_bytes", tag="hold", align_bytes=64)
+        nc.vector.tensor_copy(y_bytes[:, 0:S], x_sc[:].indirect(offs_t[:]))
+        nc.vector.tensor_copy(y_bytes[:, S : 2 * S], x_sc[:].indirect(hz_t[:]))
+        move_rows(y_planes, y_bytes, nc.sync, nc.sync)
+        x_pick = []
+        for name, lst in (("x_offs", offs_t), ("x_hz", hz_t)):
+            tile = keep.tile([P, S], U32, name=name, align_bytes=64)
+            nc.vector.tensor_copy(tile[:], x_w[:].indirect(lst[:]))
+            x_pick.append(tile)
+
+        w_dealt = []
+        for a in range(2):
+            tile = keep.tile([P, H], U32, name="w_dealt%d" % a, align_bytes=64)
+            nc.scalar.copy(
+                out=tile[:].rearrange("p (t m) -> p m t", t=PACK),
+                in_=w_raw[a][:].rearrange("p (m t) -> p m t", t=PACK),
+            )
+            w_dealt.append(tile)
+        w_sc = keep.tile([P, H], U8, name="w_sc", align_bytes=64)
+        nc.vector.tensor_copy(
+            out=w_sc[:].rearrange("p (t m) -> p m t", t=PACK),
+            in_=w_sc_raw[:].rearrange("p (m t) -> p m t", t=PACK),
+        )
+
+        n4_t = load_list(n4, "n4_t")
+        n5_t = load_list(n5, "n5_t")
+        n3_t = load_list(n3, "n3_t")
+        two_t = load_list(two, "two_t")
+        k1_t = load_list(k1, "k1_t")
+        k2_t = load_list(k2, "k2_t")
+        n6_t = load_list(n6, "n6_t")
+        n7_t = load_list(n7, "n7_t")
+        n8_t = load_list(n8, "n8_t")
+        gs_t = keep.tile([P, PACK], F32, name="gs_t")
+        nc.gpsimd.dma_start(out=gs_t[:], in_=gs.rearrange("(p t) o -> p (t o)", t=PACK))
+        d_sc = zeroed(nc.vector, G, "d_sc")
+        h_planes = zeroed(nc.vector, 2 * H + S, "h_planes")
+        nc.gpsimd.dma_start(out=d_sc[0:P:8, :].bitcast(I32), in_=d_scales[0].bitcast(I32))
+        d_w = keep.tile([P, G], U32, name="d_w", tag="hold", align_bytes=64)
+        nc.scalar.dma_start(out=d_w[:].bitcast(I32), in_=words_view(d_words))
+
+        y = []
+        for t in range(TILES):
+            m = slice(t * P, (t + 1) * P)
+            acc = psum.tile([P, S], F32, name="acc")
+            for a in range(2):
+                nc.tensor.matmul_mx(
+                    out=acc[:],
+                    lhsT=w_dealt[a][:, m].bitcast(FP8X4),
+                    lhsT_scale=w_sc[4 * a : P, m],
+                    rhs=x_pick[a][:].bitcast(FP8X4),
+                    rhs_scale=y_planes[:, a * S : (a + 1) * S],
+                    start=(a == 0),
+                    stop=(a == 1),
+                )
+            tile = keep.tile([P, S], F32, name="y%d" % t)
+            if t == 0:
+                nc.scalar.activation(tile[:], acc[:], COPY)
+            else:
+                nc.vector.tensor_copy(out=tile[:], in_=acc[:])
+            y.append(tile)
+
+        d_pick = []
+
+        def pick_bytes():
+            h_bytes = keep.tile([P, 2 * H + S], U8, name="h_bytes", tag="pb0", align_bytes=64)
+            for a, lst in enumerate((k1_t, k2_t)):
+                for c in range(0, H, S):
+                    nc.vector.tensor_copy(h_bytes[:, a * H + c : a * H + c + S], d_sc[:].indirect(cols(lst, c, S)))
+            nc.vector.tensor_copy(h_bytes[:, 2 * H : 2 * H + S], x_sc[:].indirect(two_t[:]))
+            move_rows(h_planes, h_bytes, nc.sync, nc.sync)
+
+        def pick_words():
+            tile = keep.tile([P, 2 * H + S], U32, name="d_pick", tag="pb1", align_bytes=64)
+            d_pick.append(tile)
+            nc.vector.tensor_copy(tile[:, 2 * H : 2 * H + S], x_w[:].indirect(two_t[:]))
+            for a, lst in ((1, k2_t), (0, k1_t)):
+                for c in range(0, H, S):
+                    nc.vector.tensor_copy(tile[:, a * H + c : a * H + c + S], d_w[:].indirect(cols(lst, c, S)))
+
+        z = [keep.tile([P, HALF, PACK], BF16, name="z%d" % h, align_bytes=64) for h in range(2)]
+        z_codes = keep.tile([P, S], U32, name="z_codes", align_bytes=64)
+        z_plane = keep.tile([P, S], U8, name="z_plane", align_bytes=64)
+        ub = []
+
+        def weigh(t, h, y5):
+            top = keep.tile([P, HALF], F32, name="top%d_%d" % (t, h))
+            nc.vector.tensor_max(top[:], ub[t][:, h * HALF : (h + 1) * HALF], y5)
+            nc.vector.tensor_scalar_mul(z[h][:, :, t], top[:], gs_t[:, t : t + 1])
+
+        def quantize(h):
+            c = slice(h * HALF, (h + 1) * HALF)
+            nc.vector.quantize_mx(
+                out=z_codes[:, c].bitcast(FP8X4), scales=z_plane[:, c],
+                in_=z[h][:].rearrange("p j t -> p (j t)"),
+            )
+
+        for t in range(TILES):
+            pa = keep.tile([P, W], F32, name="pa%d" % t, tag="pa%d" % t)
+            pb = keep.tile([P, W], F32, name="pb%d" % t, tag="pb%d" % t, align_bytes=64)
+            ra = keep.tile([P, W], F32, name="ra%d" % t, tag=("ra0", "d_sc", "hold", "pb2")[t], align_bytes=64)
+            y5 = keep.tile([P, HALF], F32, name="y5a%d" % t)
+            ub.append(keep.tile([P, S], F32, name="ub%d" % t))
+            nc.scalar.activation(pa[:], y[t][:].indirect(n1_t[:]), COPY)
+            nc.scalar.activation(pb[:], y[t][:].indirect(n2_t[:]), COPY)
+            nc.vector.tensor_sub(ra[:], pb[:], pa[:])
+            nc.scalar.activation(ub[t][:].indirect(n4_t[:]), pa[:], COPY)
+            nc.scalar.activation(y5[:], y[t][:].indirect(cols(n5_t, 0, HALF)), COPY)
+            nc.scalar.activation(ub[t][:].indirect(n3_t[:]), ra[:], COPY)
+            if t == 0:
+                pick_bytes()
+            if t == 1:
+                pick_words()
+            weigh(t, 0, y5[:])
+        quantize(0)
+        y5b = keep.tile([P, TILES, HALF], F32, name="y5b", tag="pa%d" % (TILES - 1))
+        for t in range(TILES):
+            nc.scalar.activation(y5b[:, t, :], y[t][:].indirect(cols(n5_t, HALF, HALF)), COPY)
+
+        def second(t, c0, n, dst):
+            m = slice(t * P, (t + 1) * P)
+            acc = psum.tile([P, n], F32, name="acc")
+            nc.tensor.matmul_mx(
+                out=acc[:], lhsT=d_pick[0][:, H + t * P : H + (t + 1) * P].bitcast(FP8X4), lhsT_scale=h_planes[:, H + t * P : H + (t + 1) * P],
+                rhs=d_pick[0][:, 2 * H + c0 : 2 * H + c0 + n].bitcast(FP8X4), rhs_scale=h_planes[:, 2 * H + c0 : 2 * H + c0 + n],
+                start=True, stop=False,
+            )
+            nc.tensor.matmul_mx(
+                out=acc[:], lhsT=d_pick[0][:, m].bitcast(FP8X4), lhsT_scale=h_planes[:, m],
+                rhs=z_codes[:, c0 : c0 + n].bitcast(FP8X4), rhs_scale=z_plane[:, c0 : c0 + n],
+                start=False, stop=True,
+            )
+            if t == 0 and c0 == 0:
+                nc.scalar.activation(dst[:, c0 : c0 + n], acc[:], COPY, scale=0.0625)
+            else:
+                nc.vector.tensor_scalar_mul(dst[:, c0 : c0 + n], acc[:], 0.0625)
+
+        h2 = [keep.tile([P, S], F32, name="h2_%d" % t) for t in range(TILES)]
+        pg = [keep.tile([P, U], F32, name="pg%d" % t) for t in range(TILES)]
+
+        def put(t, which, c0, n):
+            lst, factor = ((n6_t, 1.0), (n7_t, 0.5))[which]
+            nc.scalar.activation(pg[t][:].indirect(cols(lst, c0, n)), h2[t][:, c0 : c0 + n], COPY, scale=factor)
+
+        def finish(t, c0, n):
+            far = keep.tile([P, n], F32, name="far%d_%d" % (t, c0))
+            res = keep.tile([P, n], F32, name="res%d_%d" % (t, c0))
+            nc.scalar.activation(far[:], pg[t][:].indirect(cols(n8_t, c0, n)), COPY)
+            nc.vector.tensor_sub(res[:], pg[t][:, c0 : c0 + n], far[:])
+            nc.sync.dma_start(out=out[t * P : (t + 1) * P, c0 : c0 + n], in_=res[:])
+
+        for t in range(2):
+            second(t, 0, HALF, h2[t])
+        for t in range(TILES):
+            weigh(t, 1, y5b[:, t, :])
+        quantize(1)
+        for t in range(2):
+            second(t, HALF, HALF, h2[t])
+        for t in range(2, TILES):
+            second(t, 0, S, h2[t])
+        for c0 in (0, HALF):
+            for which in range(2):
+                for t in range(2):
+                    put(t, which, c0, HALF)
+        for which in range(2):
+            put(2, which, 0, S)
+            finish(which, 0, S)
+            put(3, which, 0, S)
+            finish(which, S, S)
+        finish(2, 0, S)
+        finish(2, S, S)
+        finish(3, 0, S)
+        finish(3, S, HALF)
+        finish(3, S + HALF, HALF)

@@ -61,7 +61,7 @@ def tile_picked_dhhzmtcphwpagtwo_none_p_kernel(
         n1_t = load_list(n1, "n1_t")
         n2_t = load_list(n2, "n2_t")
         nc.scalar.dma_start(out=x_sc[0:P:8, :].bitcast(I32), in_=x_scales[0].bitcast(I32))
-        x_w = keep.tile([P, T], U32, name="x_w", align_bytes=64)
+        x_w = keep.tile([P, T], U32, name="x_w", tag="x_w", align_bytes=64)
         nc.sync.dma_start(out=x_w[:].bitcast(I32), in_=words_view(x_words))
         w_raw = []
         for name, src in (("w1_raw", w1_words), ("w2_raw", w2_words)):
@@ -115,7 +115,7 @@ def tile_picked_dhhzmtcphwpagtwo_none_p_kernel(
         h_planes = zeroed(nc.vector, 2 * H + S, "h_planes")
         nc.gpsimd.dma_start(out=d_sc[0:P:8, :].bitcast(I32), in_=d_scales[0].bitcast(I32))
         d_w = keep.tile([P, G], U32, name="d_w", tag="hold", align_bytes=64)
-        nc.scalar.dma_start(out=d_w[:].bitcast(I32), in_=words_view(d_words))
+        nc.sync.dma_start(out=d_w[:].bitcast(I32), in_=words_view(d_words))
 
         y = []
         for t in range(TILES):
@@ -138,7 +138,7 @@ def tile_picked_dhhzmtcphwpagtwo_none_p_kernel(
                 nc.vector.tensor_copy(out=tile[:], in_=acc[:])
             y.append(tile)
 
-        d_pick = []
+        d_pick = {}
 
         def pick_bytes():
             h_bytes = keep.tile([P, 2 * H + S], U8, name="h_bytes", tag="pb0", align_bytes=64)
@@ -148,23 +148,23 @@ def tile_picked_dhhzmtcphwpagtwo_none_p_kernel(
             nc.vector.tensor_copy(h_bytes[:, 2 * H : 2 * H + S], x_sc[:].indirect(two_t[:]))
             move_rows(h_planes, h_bytes, nc.sync, nc.sync)
 
-        def pick_words():
-            tile = keep.tile([P, 2 * H + S], U32, name="d_pick", tag="pb1", align_bytes=64)
-            d_pick.append(tile)
-            nc.vector.tensor_copy(tile[:, 2 * H : 2 * H + S], x_w[:].indirect(two_t[:]))
-            for a, lst in ((1, k2_t), (0, k1_t)):
-                for c in range(0, H, S):
-                    nc.vector.tensor_copy(tile[:, a * H + c : a * H + c + S], d_w[:].indirect(cols(lst, c, S)))
+        def pick_words(a):
+            width = H + S if a == 1 else H
+            tile = keep.tile([P, width], U32, name="d_pick%d" % a, tag="pb%d" % (2 - a), align_bytes=64)
+            d_pick[a] = tile
+            for c in range(0, H, S):
+                nc.vector.tensor_copy(tile[:, c : c + S], d_w[:].indirect(cols((k1_t, k2_t)[a], c, S)))
+            if a == 1:
+                nc.vector.tensor_copy(tile[:, H : H + S], x_w[:].indirect(two_t[:]))
 
-        z = [keep.tile([P, HALF, PACK], BF16, name="z%d" % h, align_bytes=64) for h in range(2)]
+        z = [keep.tile([P, HALF, PACK], BF16, name="z%d" % h, tag="z%d" % h, align_bytes=64) for h in range(2)]
         z_codes = keep.tile([P, S], U32, name="z_codes", align_bytes=64)
         z_plane = keep.tile([P, S], U8, name="z_plane", align_bytes=64)
         ub = []
 
-        def weigh(t, h, y5):
-            top = keep.tile([P, HALF], F32, name="top%d_%d" % (t, h))
-            nc.vector.tensor_max(top[:], ub[t][:, h * HALF : (h + 1) * HALF], y5)
-            nc.vector.tensor_scalar_mul(z[h][:, :, t], top[:], gs_t[:, t : t + 1])
+        def weigh(t, h, y5, top):
+            nc.vector.tensor_max(top, ub[t][:, h * HALF : (h + 1) * HALF], y5)
+            nc.vector.tensor_scalar_mul(z[h][:, :, t], top, gs_t[:, t : t + 1])
 
         def quantize(h):
             c = slice(h * HALF, (h + 1) * HALF)
@@ -173,23 +173,32 @@ def tile_picked_dhhzmtcphwpagtwo_none_p_kernel(
                 in_=z[h][:].rearrange("p j t -> p (j t)"),
             )
 
+        y5a = keep.tile([P, TILES, HALF], F32, name="y5a")
+        ra = []
+
+        def close(t):
+            nc.scalar.activation(ub[t][:].indirect(n3_t[:]), ra[t][:], COPY)
+
         for t in range(TILES):
             pa = keep.tile([P, W], F32, name="pa%d" % t, tag="pa%d" % t)
             pb = keep.tile([P, W], F32, name="pb%d" % t, tag="pb%d" % t, align_bytes=64)
-            ra = keep.tile([P, W], F32, name="ra%d" % t, tag=("ra0", "d_sc", "hold", "pb2")[t], align_bytes=64)
-            y5 = keep.tile([P, HALF], F32, name="y5a%d" % t)
+            ra.append(keep.tile([P, W], F32, name="ra%d" % t, tag=("ra0", "d_sc", "x_w", "hold")[t], align_bytes=64))
             ub.append(keep.tile([P, S], F32, name="ub%d" % t))
             nc.scalar.activation(pa[:], y[t][:].indirect(n1_t[:]), COPY)
             nc.scalar.activation(pb[:], y[t][:].indirect(n2_t[:]), COPY)
-            nc.vector.tensor_sub(ra[:], pb[:], pa[:])
+            nc.vector.tensor_sub(ra[t][:], pb[:], pa[:])
             nc.scalar.activation(ub[t][:].indirect(n4_t[:]), pa[:], COPY)
-            nc.scalar.activation(y5[:], y[t][:].indirect(cols(n5_t, 0, HALF)), COPY)
-            nc.scalar.activation(ub[t][:].indirect(n3_t[:]), ra[:], COPY)
+            nc.scalar.activation(y5a[:, t, :], y[t][:].indirect(cols(n5_t, 0, HALF)), COPY)
             if t == 0:
                 pick_bytes()
-            if t == 1:
-                pick_words()
-            weigh(t, 0, y5[:])
+            elif t < TILES - 1:
+                pick_words(2 - t)
+            if t > 0:
+                close(t - 1)
+        close(TILES - 1)
+        top_a = keep.tile([P, TILES, HALF], F32, name="top_a", tag="pb%d" % (TILES - 1), align_bytes=64)
+        for t in range(TILES):
+            weigh(t, 0, y5a[:, t, :], top_a[:, t, :])
         quantize(0)
         y5b = keep.tile([P, TILES, HALF], F32, name="y5b", tag="pa%d" % (TILES - 1))
         for t in range(TILES):
@@ -199,8 +208,8 @@ def tile_picked_dhhzmtcphwpagtwo_none_p_kernel(
             m = slice(t * P, (t + 1) * P)
             acc = psum.tile([P, n], F32, name="acc")
             nc.tensor.matmul_mx(
-                out=acc[:], lhsT=d_pick[0][:, H + t * P : H + (t + 1) * P].bitcast(FP8X4), lhsT_scale=h_planes[:, H + t * P : H + (t + 1) * P],
-                rhs=d_pick[0][:, 2 * H + c0 : 2 * H + c0 + n].bitcast(FP8X4), rhs_scale=h_planes[:, 2 * H + c0 : 2 * H + c0 + n],
+                out=acc[:], lhsT=d_pick[1][:, m].bitcast(FP8X4), lhsT_scale=h_planes[:, H + t * P : H + (t + 1) * P],
+                rhs=d_pick[1][:, H + c0 : H + c0 + n].bitcast(FP8X4), rhs_scale=h_planes[:, 2 * H + c0 : 2 * H + c0 + n],
                 start=True, stop=False,
             )
             nc.tensor.matmul_mx(
@@ -220,17 +229,18 @@ def tile_picked_dhhzmtcphwpagtwo_none_p_kernel(
             lst, factor = ((n6_t, 1.0), (n7_t, 0.5))[which]
             nc.scalar.activation(pg[t][:].indirect(cols(lst, c0, n)), h2[t][:, c0 : c0 + n], COPY, scale=factor)
 
-        def finish(t, c0, n):
+        def finish(t, c0, n, queue=nc.sync):
             far = keep.tile([P, n], F32, name="far%d_%d" % (t, c0))
             res = keep.tile([P, n], F32, name="res%d_%d" % (t, c0))
             nc.scalar.activation(far[:], pg[t][:].indirect(cols(n8_t, c0, n)), COPY)
             nc.vector.tensor_sub(res[:], pg[t][:, c0 : c0 + n], far[:])
-            nc.sync.dma_start(out=out[t * P : (t + 1) * P, c0 : c0 + n], in_=res[:])
+            queue.dma_start(out=out[t * P : (t + 1) * P, c0 : c0 + n], in_=res[:])
 
         for t in range(2):
             second(t, 0, HALF, h2[t])
+        top_b = keep.tile([P, TILES, HALF], F32, name="top_b", tag="z0", align_bytes=64)
         for t in range(TILES):
-            weigh(t, 1, y5b[:, t, :])
+            weigh(t, 1, y5b[:, t, :], top_b[:, t, :])
         quantize(1)
         for t in range(2):
             second(t, HALF, HALF, h2[t])
@@ -248,5 +258,5 @@ def tile_picked_dhhzmtcphwpagtwo_none_p_kernel(
         finish(2, 0, S)
         finish(2, S, S)
         finish(3, 0, S)
-        finish(3, S, HALF)
-        finish(3, S + HALF, HALF)
+        finish(3, S, 192)
+        finish(3, S + 192, 64, nc.scalar)

@@ -80,11 +80,13 @@ def tile_picked_dhhzmtcphwpagtwo_none_p_kernel(
         nc.vector.tensor_copy(y_bytes[:, 0:S], x_sc[:].indirect(offs_t[:]))
         nc.vector.tensor_copy(y_bytes[:, S : 2 * S], x_sc[:].indirect(hz_t[:]))
         move_rows(y_planes, y_bytes, nc.sync, nc.sync)
-        x_pick = []
-        for name, lst in (("x_offs", offs_t), ("x_hz", hz_t)):
-            tile = keep.tile([P, S], U32, name=name, align_bytes=64)
-            nc.vector.tensor_copy(tile[:], x_w[:].indirect(lst[:]))
-            x_pick.append(tile)
+        x_pick = [keep.tile([P, S], U32, name="x_pick%d" % a, align_bytes=64) for a in range(2)]
+        w_sc = keep.tile([P, H], U8, name="w_sc", align_bytes=64)
+        w_sc_by_tile = w_sc_raw[:].rearrange("p (m t) -> p t m", t=PACK)
+        nc.vector.tensor_copy(x_pick[0][:], x_w[:].indirect(offs_t[:]))
+        nc.vector.tensor_copy(x_pick[1][:], x_w[:].indirect(hz_t[:]))
+        nc.vector.tensor_copy(out=w_sc[:, 0:P], in_=w_sc_by_tile[:, 0, :])
+        nc.vector.tensor_copy(out=w_sc[:, P:H].rearrange("p (t m) -> p t m", m=P), in_=w_sc_by_tile[:, 1:PACK, :])
 
         w_dealt = []
         for a in range(2):
@@ -94,11 +96,6 @@ def tile_picked_dhhzmtcphwpagtwo_none_p_kernel(
                 in_=w_raw[a][:].rearrange("p (m t) -> p m t", t=PACK),
             )
             w_dealt.append(tile)
-        w_sc = keep.tile([P, H], U8, name="w_sc", align_bytes=64)
-        nc.vector.tensor_copy(
-            out=w_sc[:].rearrange("p (t m) -> p m t", t=PACK),
-            in_=w_sc_raw[:].rearrange("p (m t) -> p m t", t=PACK),
-        )
 
         n4_t = load_list(n4, "n4_t")
         n5_t = load_list(n5, "n5_t")
@@ -162,8 +159,10 @@ def tile_picked_dhhzmtcphwpagtwo_none_p_kernel(
         z_plane = keep.tile([P, S], U8, name="z_plane", align_bytes=64)
         ub = []
 
-        def weigh(t, h, y5, top):
+        def larger(t, h, y5, top):
             nc.vector.tensor_max(top, ub[t][:, h * HALF : (h + 1) * HALF], y5)
+
+        def weigh(t, h, top):
             nc.vector.tensor_scalar_mul(z[h][:, :, t], top, gs_t[:, t : t + 1])
 
         def quantize(h):
@@ -198,7 +197,8 @@ def tile_picked_dhhzmtcphwpagtwo_none_p_kernel(
         close(TILES - 1)
         top_a = keep.tile([P, TILES, HALF], F32, name="top_a", tag="pb%d" % (TILES - 1), align_bytes=64)
         for t in range(TILES):
-            weigh(t, 0, y5a[:, t, :], top_a[:, t, :])
+            larger(t, 0, y5a[:, t, :], top_a[:, t, :])
+            weigh(t, 0, top_a[:, t, :])
         quantize(0)
         y5b = keep.tile([P, TILES, HALF], F32, name="y5b", tag="pa%d" % (TILES - 1))
         for t in range(TILES):
@@ -223,7 +223,7 @@ def tile_picked_dhhzmtcphwpagtwo_none_p_kernel(
                 nc.vector.tensor_scalar_mul(dst[:, c0 : c0 + n], acc[:], 0.0625)
 
         h2 = [keep.tile([P, S], F32, name="h2_%d" % t) for t in range(TILES)]
-        pg = [keep.tile([P, U], F32, name="pg%d" % t) for t in range(TILES)]
+        pg = [keep.tile([P, U + 16], F32, name="pg%d" % t) for t in range(TILES)]
 
         def put(t, which, c0, n):
             lst, factor = ((n6_t, 1.0), (n7_t, 0.5))[which]
@@ -240,7 +240,9 @@ def tile_picked_dhhzmtcphwpagtwo_none_p_kernel(
             second(t, 0, HALF, h2[t])
         top_b = keep.tile([P, TILES, HALF], F32, name="top_b", tag="z0", align_bytes=64)
         for t in range(TILES):
-            weigh(t, 1, y5b[:, t, :], top_b[:, t, :])
+            larger(t, 1, y5b[:, t, :], top_b[:, t, :])
+        for t in range(TILES):
+            weigh(t, 1, top_b[:, t, :])
         quantize(1)
         for t in range(2):
             second(t, HALF, HALF, h2[t])
@@ -250,13 +252,14 @@ def tile_picked_dhhzmtcphwpagtwo_none_p_kernel(
             for which in range(2):
                 for t in range(2):
                     put(t, which, c0, HALF)
-        for which in range(2):
-            put(2, which, 0, S)
-            finish(which, 0, S)
-            put(3, which, 0, S)
-            finish(which, S, S)
-        finish(2, 0, S)
-        finish(2, S, S)
+        put(2, 0, 0, S)
+        finish(0, 0, U)
+        put(2, 1, 0, S)
+        finish(1, 0, U)
+        put(3, 0, 0, S)
+        finish(2, 0, 384)
+        put(3, 1, 0, S)
+        finish(2, 384, 128)
         finish(3, 0, S)
         finish(3, S, 192)
         finish(3, S + 192, 64, nc.scalar)

@@ -48,10 +48,9 @@ def tile_picked_dhhzmtcphwpagtwo_none_p_kernel(
             eng.memset(tile[:].bitcast(I32), 0)
             return tile
 
-        def move_rows(dst, src, one, other):
-            for r in range(4):
-                eng = one if r % 2 == 0 else other
-                eng.dma_start(out=dst[r:P:32, :].bitcast(I32), in_=src[8 * r : P : 32, :].bitcast(I32))
+        def move_rows(dst, src, first):
+            for r in range(first, 4):
+                nc.sync.dma_start(out=dst[r:P:32, :].bitcast(I32), in_=src[8 * r : P : 32, :].bitcast(I32))
 
         x_sc = zeroed(nc.vector, T, "x_sc")
         w_sc_raw = zeroed(nc.vector, H, "w_sc_raw")
@@ -66,7 +65,7 @@ def tile_picked_dhhzmtcphwpagtwo_none_p_kernel(
         w_raw = []
         for name, src in (("w1_raw", w1_words), ("w2_raw", w2_words)):
             tile = keep.tile([P, H], U32, name=name, align_bytes=64)
-            nc.sync.dma_start(out=tile[:].bitcast(I32), in_=words_view(src))
+            nc.gpsimd.dma_start(out=tile[:].bitcast(I32), in_=words_view(src))
             w_raw.append(tile)
         for a, src in enumerate((w1_scales, w2_scales)):
             for q in range(4):
@@ -79,7 +78,7 @@ def tile_picked_dhhzmtcphwpagtwo_none_p_kernel(
         y_bytes = keep.tile([P, 2 * S], U8, name="y_bytes", tag="hold", align_bytes=64)
         nc.vector.tensor_copy(y_bytes[:, 0:S], x_sc[:].indirect(offs_t[:]))
         nc.vector.tensor_copy(y_bytes[:, S : 2 * S], x_sc[:].indirect(hz_t[:]))
-        move_rows(y_planes, y_bytes, nc.sync, nc.sync)
+        move_rows(y_planes, y_bytes, 0)
         x_pick = [keep.tile([P, S], U32, name="x_pick%d" % a, align_bytes=64) for a in range(2)]
         w_sc = keep.tile([P, H], U8, name="w_sc", align_bytes=64)
         w_sc_by_tile = w_sc_raw[:].rearrange("p (m t) -> p t m", t=PACK)
@@ -114,26 +113,30 @@ def tile_picked_dhhzmtcphwpagtwo_none_p_kernel(
         d_w = keep.tile([P, G], U32, name="d_w", tag="hold", align_bytes=64)
         nc.sync.dma_start(out=d_w[:].bitcast(I32), in_=words_view(d_words))
 
-        y = []
-        for t in range(TILES):
+        y = [keep.tile([P, S], F32, name="y%d" % t) for t in range(TILES)]
+
+        def first(t, c0, n):
             m = slice(t * P, (t + 1) * P)
-            acc = psum.tile([P, S], F32, name="acc")
+            acc = psum.tile([P, n], F32, name="acc")
             for a in range(2):
                 nc.tensor.matmul_mx(
                     out=acc[:],
                     lhsT=w_dealt[a][:, m].bitcast(FP8X4),
                     lhsT_scale=w_sc[4 * a : P, m],
-                    rhs=x_pick[a][:].bitcast(FP8X4),
-                    rhs_scale=y_planes[:, a * S : (a + 1) * S],
+                    rhs=x_pick[a][:, c0 : c0 + n].bitcast(FP8X4),
+                    rhs_scale=y_planes[:, a * S + c0 : a * S + c0 + n],
                     start=(a == 0),
                     stop=(a == 1),
                 )
-            tile = keep.tile([P, S], F32, name="y%d" % t)
             if t == 0:
-                nc.scalar.activation(tile[:], acc[:], COPY)
+                nc.scalar.activation(y[t][:, c0 : c0 + n], acc[:], COPY)
             else:
-                nc.vector.tensor_copy(out=tile[:], in_=acc[:])
-            y.append(tile)
+                nc.vector.tensor_copy(out=y[t][:, c0 : c0 + n], in_=acc[:])
+
+        first(0, 0, HALF)
+        first(0, HALF, HALF)
+        for t in range(1, TILES):
+            first(t, 0, S)
 
         d_pick = {}
 
@@ -143,7 +146,7 @@ def tile_picked_dhhzmtcphwpagtwo_none_p_kernel(
                 for c in range(0, H, S):
                     nc.vector.tensor_copy(h_bytes[:, a * H + c : a * H + c + S], d_sc[:].indirect(cols(lst, c, S)))
             nc.vector.tensor_copy(h_bytes[:, 2 * H : 2 * H + S], x_sc[:].indirect(two_t[:]))
-            move_rows(h_planes, h_bytes, nc.sync, nc.sync)
+            move_rows(h_planes, h_bytes, 0)
 
         def pick_words(a):
             width = H + S if a == 1 else H

from contextlib import ExitStack

import concourse.mybir as mybir

K, T, S, H, W, G, U = 512, 1024, 256, 512, 128, 2048, 512
FLOPS = 4 * 2 * K * H * S

F32 = mybir.dt.float32
BF16 = mybir.dt.bfloat16
I32 = mybir.dt.int32
U32 = mybir.dt.uint32
U16 = mybir.dt.uint16
U8 = mybir.dt.uint8
FP8X4 = mybir.dt.float8_e4m3fn_x4
COPY = mybir.ActivationFunctionType.Copy

P = 128
PACK = 4
TILES = H // P
HALF = S // 2


def words_view(ap):
    return ap[0].rearrange("p n t -> p (n t)").bitcast(I32)


def cols(lst, start, count):
    return lst[:, start // 16 : (start + count) // 16]


def tile_picked_dhhzmtcphwpagtwo_none_p_kernel(
    tc, x_words, x_scales, w1_words, w1_scales, w2_words, w2_scales, gs, d_words, d_scales,
    offs, hz, n1, n2, n3, n4, n5, k1, k2, two, n6, n7, n8, out,
):
    nc = tc.nc
    with ExitStack() as ctx:
        lists = ctx.enter_context(tc.tile_pool(name="lists", bufs=1))
        keep = ctx.enter_context(tc.tile_pool(name="keep", bufs=1))
        psum = ctx.enter_context(tc.psum_pool(name="psum", bufs=8))

        def load_list(src, name):
            tile = lists.tile(list(src.shape), U16, name=name)
            nc.sync.dma_start(tile[:], src)
            return tile

        def zeroed(eng, width, name):
            tile = keep.tile([P, width], U8, name=name, tag=name, align_bytes=64)
            eng.memset(tile[:].bitcast(I32), 0)
            return tile

        def move_rows(dst, src, first):
            for r in range(first, 4):
                nc.sync.dma_start(out=dst[r:P:32, :].bitcast(I32), in_=src[8 * r : P : 32, :].bitcast(I32))

        x_sc = zeroed(nc.vector, T, "x_sc")
        w_sc_raw = zeroed(nc.vector, H, "w_sc_raw")
        y_planes = zeroed(nc.vector, 2 * S, "y_planes")
        offs_t = load_list(offs, "offs_t")
        hz_t = load_list(hz, "hz_t")
        n1_t = load_list(n1, "n1_t")
        n2_t = load_list(n2, "n2_t")
        nc.scalar.dma_start(out=x_sc[0:P:8, :].bitcast(I32), in_=x_scales[0].bitcast(I32))
        x_w = keep.tile([P, T], U32, name="x_w", tag="x_w", align_bytes=64)
        nc.sync.dma_start(out=x_w[:].bitcast(I32), in_=words_view(x_words))
        w_raw = []
        for name, src in (("w1_raw", w1_words), ("w2_raw", w2_words)):
            tile = keep.tile([P, H], U32, name=name, align_bytes=64)
            nc.gpsimd.dma_start(out=tile[:].bitcast(I32), in_=words_view(src))
            w_raw.append(tile)
        for a, src in enumerate((w1_scales, w2_scales)):
            for q in range(4):
                eng = nc.sync
                eng.dma_start(
                    out=w_sc_raw[32 * q + 4 * a : 32 * q + 4 * a + 4, :].bitcast(I32),
                    in_=src[0, 4 * q : 4 * q + 4, :].bitcast(I32),
                )

        y_bytes = keep.tile([P, 2 * S], U8, name="y_bytes", tag="hold", align_bytes=64)
        nc.vector.tensor_copy(y_bytes[:, 0:S], x_sc[:].indirect(offs_t[:]))
        nc.vector.tensor_copy(y_bytes[:, S : 2 * S], x_sc[:].indirect(hz_t[:]))
        move_rows(y_planes, y_bytes, 0)
        x_pick = [keep.tile([P, S], U32, name="x_pick%d" % a, align_bytes=64) for a in range(2)]
        w_sc = keep.tile([P, H], U8, name="w_sc", align_bytes=64)
        w_sc_by_tile = w_sc_raw[:].rearrange("p (m t) -> p t m", t=PACK)
        nc.vector.tensor_copy(x_pick[0][:], x_w[:].indirect(offs_t[:]))
        nc.vector.tensor_copy(x_pick[1][:], x_w[:].indirect(hz_t[:]))
        nc.vector.tensor_copy(out=w_sc[:, 0:P], in_=w_sc_by_tile[:, 0, :])
        nc.vector.tensor_copy(out=w_sc[:, P:H].rearrange("p (t m) -> p t m", m=P), in_=w_sc_by_tile[:, 1:PACK, :])

        w_dealt = []
        for a in range(2):
            tile = keep.tile([P, H], U32, name="w_dealt%d" % a, align_bytes=64)
            nc.scalar.copy(
                out=tile[:].rearrange("p (t m) -> p m t", t=PACK),
                in_=w_raw[a][:].rearrange("p (m t) -> p m t", t=PACK),
            )
            w_dealt.append(tile)

        n4_t = load_list(n4, "n4_t")
        n5_t = load_list(n5, "n5_t")
        n3_t = load_list(n3, "n3_t")
        two_t = load_list(two, "two_t")
        k1_t = load_list(k1, "k1_t")
        k2_t = load_list(k2, "k2_t")
        n6_t = load_list(n6, "n6_t")
        n7_t = load_list(n7, "n7_t")
        n8_t = load_list(n8, "n8_t")
        gs_t = keep.tile([P, PACK], F32, name="gs_t")
        nc.gpsimd.dma_start(out=gs_t[:], in_=gs.rearrange("(p t) o -> p (t o)", t=PACK))
        d_sc = zeroed(nc.vector, G, "d_sc")
        h_planes = zeroed(nc.vector, 2 * H + S, "h_planes")
        nc.gpsimd.dma_start(out=d_sc[0:P:8, :].bitcast(I32), in_=d_scales[0].bitcast(I32))
        d_w = keep.tile([P, G], U32, name="d_w", tag="hold", align_bytes=64)
        nc.sync.dma_start(out=d_w[:].bitcast(I32), in_=words_view(d_words))

        y = [keep.tile([P, S], F32, name="y%d" % t) for t in range(TILES)]

        def first(t, c0, n):
            m = slice(t * P, (t + 1) * P)
            acc = psum.tile([P, n], F32, name="acc")
            for a in range(2):
                nc.tensor.matmul_mx(
                    out=acc[:],
                    lhsT=w_dealt[a][:, m].bitcast(FP8X4),
                    lhsT_scale=w_sc[4 * a : P, m],
                    rhs=x_pick[a][:, c0 : c0 + n].bitcast(FP8X4),
                    rhs_scale=y_planes[:, a * S + c0 : a * S + c0 + n],
                    start=(a == 0),
                    stop=(a == 1),
                )
            if t == 0:
                nc.scalar.activation(y[t][:, c0 : c0 + n], acc[:], COPY)
            else:
                nc.vector.tensor_copy(out=y[t][:, c0 : c0 + n], in_=acc[:])

        first(0, 0, HALF)
        first(0, HALF, HALF)
        for t in range(1, TILES):
            first(t, 0, S)

        d_pick = {}

        def pick_bytes():
            h_bytes = keep.tile([P, 2 * H + S], U8, name="h_bytes", tag="pb0", align_bytes=64)
            for a, lst in enumerate((k1_t, k2_t)):
                for c in range(0, H, S):
                    nc.vector.tensor_copy(h_bytes[:, a * H + c : a * H + c + S], d_sc[:].indirect(cols(lst, c, S)))
            nc.vector.tensor_copy(h_bytes[:, 2 * H : 2 * H + S], x_sc[:].indirect(two_t[:]))
            move_rows(h_planes, h_bytes, 0)

        def pick_words(a):
            width = H + S if a == 1 else H
            tile = keep.tile([P, width], U32, name="d_pick%d" % a, tag="pb%d" % (2 - a), align_bytes=64)
            d_pick[a] = tile
            for c in range(0, H, S):
                nc.vector.tensor_copy(tile[:, c : c + S], d_w[:].indirect(cols((k1_t, k2_t)[a], c, S)))
            if a == 1:
                nc.vector.tensor_copy(tile[:, H : H + S], x_w[:].indirect(two_t[:]))

        z = [keep.tile([P, HALF, PACK], BF16, name="z%d" % h, tag="z%d" % h, align_bytes=64) for h in range(2)]
        z_codes = keep.tile([P, S], U32, name="z_codes", align_bytes=64)
        z_plane = keep.tile([P, S], U8, name="z_plane", align_bytes=64)
        ub = []

        def larger(t, h, y5, top):
            nc.vector.tensor_max(top, ub[t][:, h * HALF : (h + 1) * HALF], y5)

        def weigh(t, h, top):
            nc.vector.tensor_scalar_mul(z[h][:, :, t], top, gs_t[:, t : t + 1])

        def quantize(h):
            c = slice(h * HALF, (h + 1) * HALF)
            nc.vector.quantize_mx(
                out=z_codes[:, c].bitcast(FP8X4), scales=z_plane[:, c],
                in_=z[h][:].rearrange("p j t -> p (j t)"),
            )

        y5a = keep.tile([P, TILES, HALF], F32, name="y5a")
        ra = []

        def close(t):
            nc.scalar.activation(ub[t][:].indirect(n3_t[:]), ra[t][:], COPY)

        for t in range(TILES):
            pa = keep.tile([P, W], F32, name="pa%d" % t, tag="pa%d" % t)
            pb = keep.tile([P, W], F32, name="pb%d" % t, tag="pb%d" % t, align_bytes=64)
            ra.append(keep.tile([P, W], F32, name="ra%d" % t, tag=("ra0", "d_sc", "x_w", "hold")[t], align_bytes=64))
            ub.append(keep.tile([P, S], F32, name="ub%d" % t))
            nc.scalar.activation(pa[:], y[t][:].indirect(n1_t[:]), COPY)
            nc.scalar.activation(pb[:], y[t][:].indirect(n2_t[:]), COPY)
            nc.vector.tensor_sub(ra[t][:], pb[:], pa[:])
            nc.scalar.activation(ub[t][:].indirect(n4_t[:]), pa[:], COPY)
            nc.scalar.activation(y5a[:, t, :], y[t][:].indirect(cols(n5_t, 0, HALF)), COPY)
            if t == 0:
                pick_bytes()
            elif t < TILES - 1:
                pick_words(2 - t)
            if t > 0:
                close(t - 1)
        close(TILES - 1)
        top_a = keep.tile([P, TILES, HALF], F32, name="top_a", tag="pb%d" % (TILES - 1), align_bytes=64)
        for t in range(TILES):
            larger(t, 0, y5a[:, t, :], top_a[:, t, :])
            weigh(t, 0, top_a[:, t, :])
        quantize(0)
        y5b = keep.tile([P, TILES, HALF], F32, name="y5b", tag="pa%d" % (TILES - 1))
        for t in range(TILES):
            nc.scalar.activation(y5b[:, t, :], y[t][:].indirect(cols(n5_t, HALF, HALF)), COPY)

        def second(t, c0, n, dst):
            m = slice(t * P, (t + 1) * P)
            acc = psum.tile([P, n], F32, name="acc")
            nc.tensor.matmul_mx(
                out=acc[:], lhsT=d_pick[1][:, m].bitcast(FP8X4), lhsT_scale=h_planes[:, H + t * P : H + (t + 1) * P],
                rhs=d_pick[1][:, H + c0 : H + c0 + n].bitcast(FP8X4), rhs_scale=h_planes[:, 2 * H + c0 : 2 * H + c0 + n],
                start=True, stop=False,
            )
            nc.tensor.matmul_mx(
                out=acc[:], lhsT=d_pick[0][:, m].bitcast(FP8X4), lhsT_scale=h_planes[:, m],
                rhs=z_codes[:, c0 : c0 + n].bitcast(FP8X4), rhs_scale=z_plane[:, c0 : c0 + n],
                start=False, stop=True,
            )
            if t == 0 and c0 == 0:
                nc.scalar.activation(dst[:, c0 : c0 + n], acc[:], COPY, scale=0.0625)
            else:
                nc.vector.tensor_scalar_mul(dst[:, c0 : c0 + n], acc[:], 0.0625)

        h2 = [keep.tile([P, S], F32, name="h2_%d" % t) for t in range(TILES)]
        pg = [keep.tile([P, U + 16], F32, name="pg%d" % t) for t in range(TILES)]

        def put(t, which, c0, n):
            lst, factor = ((n6_t, 1.0), (n7_t, 0.5))[which]
            nc.scalar.activation(pg[t][:].indirect(cols(lst, c0, n)), h2[t][:, c0 : c0 + n], COPY, scale=factor)

        def finish(t, c0, n, queue=nc.sync):
            far = keep.tile([P, n], F32, name="far%d_%d" % (t, c0))
            res = keep.tile([P, n], F32, name="res%d_%d" % (t, c0))
            nc.scalar.activation(far[:], pg[t][:].indirect(cols(n8_t, c0, n)), COPY)
            nc.vector.tensor_sub(res[:], pg[t][:, c0 : c0 + n], far[:])
            queue.dma_start(out=out[t * P : (t + 1) * P, c0 : c0 + n], in_=res[:])

        for t in range(2):
            second(t, 0, HALF, h2[t])
        top_b = keep.tile([P, TILES, HALF], F32, name="top_b", tag="z0", align_bytes=64)
        for t in range(TILES):
            larger(t, 1, y5b[:, t, :], top_b[:, t, :])
        for t in range(TILES):
            weigh(t, 1, top_b[:, t, :])
        quantize(1)
        for t in range(2):
            second(t, HALF, HALF, h2[t])
        for t in range(2, TILES):
            second(t, 0, S, h2[t])
        for c0 in (0, HALF):
            for which in range(2):
                for t in range(2):
                    put(t, which, c0, HALF)
        put(2, 0, 0, S)
        finish(0, 0, U)
        put(2, 1, 0, S)
        finish(1, 0, U)
        put(3, 0, 0, S)
        finish(2, 0, 384)
        put(3, 1, 0, S)
        finish(2, 384, 128)
        finish(3, 0, S)
        finish(3, S, 192)
        finish(3, S + 192, 64, nc.scalar)
